import numpy as np
import ml_dtypes


def mxq(x, axis, fmt="e4m3"):
    dtype, down = {"e4m3": (ml_dtypes.float8_e4m3fn, 7), "e5m2": (ml_dtypes.float8_e5m2, 14)}[fmt]
    v = np.moveaxis(np.asarray(x, np.float32).astype(ml_dtypes.bfloat16).astype(np.float64), axis, -1)
    blocks = v.reshape(v.shape[:-1] + (-1, 32))
    amax = np.abs(blocks).max(-1, keepdims=True)
    byte = np.maximum(np.where(amax > 0, np.frexp(amax)[1] - 1 + 127, 0) - down, 1)
    scale = np.exp2(byte - 127.0)
    codes = (blocks / scale).astype(np.float32).astype(dtype).astype(np.float64)
    return np.moveaxis((codes * scale).reshape(v.shape), -1, axis)


WIDE = False


def mx_kscale(k):
    if not WIDE:
        return np.ones(k)
    levels = np.array([10, -10, 5, -5, 0])
    if k % 512:
        return np.exp2(np.random.permutation(np.resize(levels, k // 32))).repeat(32)
    a = np.empty((k // 512, 16))
    for p in range(k // 512):
        a[p, :8] = np.random.permutation(np.resize(levels, 8))
        for g in range(8):
            far = levels[np.abs(levels - a[p, g]) >= 10]
            a[p, g + 8] = far[np.random.randint(len(far))]
    return np.exp2(a.ravel()).repeat(32)


BF16 = ml_dtypes.bfloat16


def bf(x):
    return np.asarray(x, np.float32).astype(BF16)


def f64(x):
    return np.asarray(x).astype(np.float64)


E2M1 = np.array([0.0, 0.5, 1.0, 1.5, 2.0, 3.0, 4.0, 6.0, -0.0, -0.5, -1.0, -1.5, -2.0, -3.0, -4.0, -6.0])


def pack_weight(w, fmt):
    k, n = w.shape
    w = f64(bf(w)).reshape(k // 32, 32, n)
    amax = np.abs(w).max(1)
    if fmt == "e4m3":
        byte = np.frexp(amax)[1] - 1 + 127 - 7
    else:
        mant, ex = np.frexp(amax / 6.0)
        byte = np.where(mant > 0.5, ex, ex - 1) + 127
    byte = np.clip(np.where(amax > 0, byte, 1), 1, 254)
    scaled = (w * np.exp2(127.0 - byte)[:, None, :]).reshape(k, n).astype(np.float32)
    by_word = np.ascontiguousarray(scaled.reshape(k // 512, 128, 4, n).transpose(0, 1, 3, 2))
    if fmt == "e4m3":
        words = by_word.astype(ml_dtypes.float8_e4m3fn).view(np.uint8)
    else:
        c = by_word.astype(ml_dtypes.float4_e2m1fn).view(np.uint8) & 0xF
        words = c[..., 0::2] | (c[..., 1::2] << 4)
    return np.ascontiguousarray(words), np.ascontiguousarray(byte.astype(np.uint8).reshape(k // 512, 16, n))


def unpack_weight(words, scales, fmt):
    g, p, n, _ = words.shape
    if fmt == "e4m3":
        vals = np.ascontiguousarray(words).view(ml_dtypes.float8_e4m3fn).astype(np.float64)
    else:
        nib = np.empty((g, p, n, 4), np.uint8)
        nib[..., 0::2] = words & 0xF
        nib[..., 1::2] = words >> 4
        vals = E2M1[nib]
    vals = vals * np.repeat(np.exp2(scales.astype(np.float64) - 127.0), 8, axis=1)[..., None]
    return vals.transpose(0, 1, 3, 2).reshape(g * 512, n)
def pack4(w):
    words, scales = pack_weight(w, "e2m1")
    return words.reshape(words.shape[0], 128, -1), scales


def unpack4(words, scales):
    return unpack_weight(words.reshape(words.shape[0], 128, -1, 2), scales, "e2m1")


def planes(Y):
    n, m = Y.shape
    b = f64(bf(Y)).reshape(n // 32, 32, m)
    amax = np.abs(b).max(1)
    byte = np.clip(np.where(amax > 0, np.frexp(amax)[1] - 1 + 127 - 7, 1), 1, 254)
    codes = (b * np.exp2(127.0 - byte)[:, None, :]).reshape(n, m).astype(np.float32).astype(ml_dtypes.float8_e4m3fn).view(np.uint8)
    words = codes.reshape(n // 512, 128, 4, m).transpose(0, 1, 3, 2)
    return np.ascontiguousarray(words), np.ascontiguousarray(byte.astype(np.uint8).reshape(n // 512, 16, m))


SPOTS, GENES = 1536, 512
NEAR, MID, FAR = (0.0, 0.05), (0.2, 0.06), (0.45, 0.08)


def spatial_weights(d, radius, width):
    w = (1.0 - np.eye(SPOTS)) / (1.0 + ((d - radius) / width) ** 2)
    return w / np.sqrt((w * w).sum(axis=0, keepdims=True))


def setup_inputs():
    s = mx_kscale(SPOTS)[:, None]
    px, py = np.random.rand(SPOTS), np.random.rand(SPOTS)
    d = np.hypot(px[:, None] - px[None, :], py[:, None] - py[None, :])
    site = np.exp(0.8 * np.random.randn(SPOTS))
    z = np.random.randn(SPOTS, GENES)
    z = z - z.mean(axis=0, keepdims=True)
    z_words, z_scales = pack_weight(z * s, "e4m3")
    near = bf(spatial_weights(d, *NEAR) * site / s)
    mid_words, mid_scales = pack_weight(spatial_weights(d, *MID) * site / s, "e4m3")
    far_words, far_scales = pack4(spatial_weights(d, *FAR) * site / s)
    r_mid = bf(np.exp(0.4 * np.random.randn(GENES)))
    r_far = bf(np.exp(0.4 * np.random.randn(GENES)))
    return {"z_words": z_words, "z_scales": z_scales, "near": near,
            "mid_words": mid_words, "mid_scales": mid_scales,
            "far_words": far_words, "far_scales": far_scales,
            "r_mid": r_mid, "r_far": r_far}


def reference(z_words, z_scales, near, mid_words, mid_scales, far_words, far_scales, r_mid, r_far):
    z = unpack_weight(z_words, z_scales, "e4m3")
    a = mxq(f64(near), 0, "e4m3")
    b = unpack_weight(mid_words, mid_scales, "e4m3")
    c = unpack4(far_words, far_scales)
    lag_near = a.T @ z
    lag_mid = b.T @ z
    lag_far = c.T @ z
    y = lag_near + f64(r_mid) * lag_mid + f64(r_far) * lag_far
    Y = y.reshape(SPOTS, GENES)
    words, scales = planes(Y)
    return y, words, scales

@@ -1,0 +1,358 @@
+from contextlib import ExitStack
+
+import concourse.mybir as mybir
+from concourse.masks import make_identity
+
+SPOTS, GENES = 1536, 512
+FLOPS = 3 * 2 * SPOTS * SPOTS * GENES
+
+F32 = mybir.dt.float32
+BF16 = mybir.dt.bfloat16
+I32 = mybir.dt.int32
+U32 = mybir.dt.uint32
+U8 = mybir.dt.uint8
+FP8X4 = mybir.dt.float8_e4m3fn_x4
+FP4X4 = mybir.dt.float4_e2m1fn_x4
+COPY = mybir.ActivationFunctionType.Copy
+MULT = mybir.AluOpType.mult
+ADD = mybir.AluOpType.add
+
+P = 128
+PACK = 4
+CHUNK = P * PACK
+PASSES = SPOTS // CHUNK
+CHUNKS = SPOTS // CHUNK
+BLOCKS = GENES // P
+QUADS = 4
+MID_ROW = 4
+
+
+def tile_moran_three_range_lag_k3_kernel(
+    tc, z_words, z_scales, near, mid_words, mid_scales, far_words, far_scales, r_mid, r_far,
+    out_0, out_1, out_2,
+):
+    nc = tc.nc
+    with ExitStack() as ctx:
+        keep = ctx.enter_context(tc.tile_pool(name="keep", bufs=1))
+        work = ctx.enter_context(tc.tile_pool(name="work", bufs=2))
+        psum = ctx.enter_context(tc.psum_pool(name="psum", bufs=8))
+        ctx.enter_context(tc.manual_schedule())
+
+        def keep_tile(shape, dtype, name):
+            return keep.tile(shape, dtype, name=name, align_bytes=64)
+
+        def new_bank():
+            return psum.tile([P, CHUNK], F32, name="bank", tag="bank")
+
+        z_codes = [keep_tile([P, GENES], U32, f"z_codes{g}") for g in range(PASSES)]
+        mid_first = [keep_tile([P, CHUNK], U32, f"mid_first{g}") for g in range(PASSES)]
+        mid_later = [keep_tile([P, PASSES, CHUNK], U32, f"mid_later{c}") for c in range(1, CHUNKS)]
+        far_codes = [keep_tile([P, PASSES, 2 * CHUNK], U8, f"far_codes{c}") for c in range(CHUNKS)]
+        near_raw = {(c, g): keep_tile([P, PACK, CHUNK], BF16, f"near_raw{c}{g}")
+                    for c in range(CHUNKS) for g in range(PASSES)}
+        near_codes = {(c, g): keep_tile([P, CHUNK], U32, f"near_codes{c}{g}")
+                      for c in range(CHUNKS) for g in range(PASSES)}
+        near_plane = {(c, g): keep_tile([P, CHUNK], U8, f"near_plane{c}{g}")
+                      for c in range(CHUNKS) for g in range(PASSES)}
+        z_plane = keep_tile([P, PASSES * GENES], U8, "z_plane")
+        mid_plane_first = keep_tile([P, PASSES * CHUNK], U8, "mid_plane_first")
+        later = SPOTS - CHUNK
+        mid_plane_later = keep_tile([P, PASSES * later], U8, "mid_plane_later")
+        far_plane = keep_tile([P, PASSES * SPOTS], U8, "far_plane")
+        r_mid_raw = keep_tile([P, BLOCKS, 2], BF16, "r_mid_raw")
+        r_far_raw = keep_tile([P, BLOCKS, 2], BF16, "r_far_raw")
+        r_mid_col = keep_tile([P, BLOCKS], F32, "r_mid_col")
+        ident = keep_tile([P, P], F32, "ident")
+        y_codes = keep_tile([P, CHUNKS, GENES], U32, "y_codes")
+        y_plane = keep_tile([P, CHUNKS, GENES], U8, "y_plane")
+        y = [keep_tile([P, PACK, GENES], F32, f"y{c}") for c in range(CHUNKS)]
+
+        def cols(c):
+            return slice(c * CHUNK, (c + 1) * CHUNK)
+
+        def load_plane(queue, plane, first_row, scales, col0, width, quads):
+            for q in quads:
+                row = 32 * q + first_row
+                queue.dma_start(
+                    out=plane[row:row + 4, 0:PASSES * width].rearrange("r (g n) -> r g n", g=PASSES).bitcast(I32),
+                    in_=scales[:, 4 * q:4 * q + 4, col0:col0 + width].rearrange("g r n -> r g n").bitcast(I32),
+                )
+
+        def load_z(queue, g):
+            queue.dma_start(out=z_codes[g][:].bitcast(I32),
+                            in_=z_words[g].rearrange("p n t -> p (n t)").bitcast(I32))
+
+        def load_mid_first(queue, g):
+            queue.dma_start(out=mid_first[g][:].bitcast(I32),
+                            in_=mid_words[g, :, cols(0), :].rearrange("p n t -> p (n t)").bitcast(I32))
+
+        def load_mid(c):
+            nc.sync.dma_start(out=mid_later[c - 1][:].bitcast(I32),
+                              in_=mid_words[:, :, cols(c), :].rearrange("g p n t -> p g (n t)").bitcast(I32))
+
+        def load_far(c):
+            nc.sync.dma_start(out=far_codes[c][:].bitcast(I32),
+                              in_=far_words[:, :, 2 * CHUNK * c:2 * CHUNK * (c + 1)].rearrange("g p b -> p g b").bitcast(I32))
+
+        def load_near(c, g):
+            nc.sync.dma_start(out=near_raw[c, g][:],
+                              in_=near[cols(g), cols(c)].rearrange("(p j) w -> p j w", j=PACK))
+
+        nc.vector.memset(z_plane[:].bitcast(I32), 0)
+        nc.vector.memset(mid_plane_first[:].bitcast(I32), 0)
+        nc.vector.memset(far_plane[:, 0:PASSES * SPOTS].bitcast(I32), 0)
+        nc.vector.memset(mid_plane_later[:, 0:PASSES * later].bitcast(I32), 0)
+
+        with nc.allow_non_contiguous_dma(reason="one range weight to a partition"):
+            nc.gpsimd.dma_start(out=r_mid_raw[:, :, 0], in_=r_mid.rearrange("(b p) -> p b", p=P))
+            nc.gpsimd.dma_start(out=r_far_raw[:, :, 0], in_=r_far.rearrange("(b p) -> p b", p=P))
+        make_identity(nc, ident[:])
+
+        load_plane(nc.sync, z_plane, 0, z_scales, 0, GENES, range(4))
+        load_z(nc.sync, 0)
+        load_mid_first(nc.sync, 0)
+        load_plane(nc.sync, mid_plane_first, MID_ROW, mid_scales, 0, CHUNK, range(4))
+        for g in range(1, PASSES):
+            load_z(nc.sync, g)
+            load_mid_first(nc.sync, g)
+        load_plane(nc.sync, far_plane, 0, far_scales, 0, SPOTS, range(4))
+        load_far(0)
+        load_near(0, 0)
+        load_mid(1)
+        load_plane(nc.sync, mid_plane_later, MID_ROW, mid_scales, CHUNK, later, range(4))
+        load_near(0, 1)
+        load_near(0, 2)
+        load_far(1)
+        for g in range(PASSES):
+            load_near(1, g)
+        load_mid(2)
+        load_near(2, 0)
+        load_near(2, 1)
+        load_far(2)
+        load_near(2, 2)
+
+        nc.scalar.copy(out=r_mid_col[:], in_=r_mid_raw[:, :, 0])
+
+        def z_block(g, b):
+            return (z_codes[g][:, b * P:(b + 1) * P].bitcast(FP8X4),
+                    z_plane[:, g * GENES + b * P:g * GENES + (b + 1) * P])
+
+        def mid_operand(c, g):
+            if c == 0:
+                return mid_first[g][:].bitcast(FP8X4), mid_plane_first[MID_ROW:P, g * CHUNK:(g + 1) * CHUNK]
+            start = g * later + (c - 1) * CHUNK
+            return mid_later[c - 1][:, g, :].bitcast(FP8X4), mid_plane_later[MID_ROW:P, start:start + CHUNK]
+
+        def far_operand(c, g):
+            start = g * SPOTS + c * CHUNK
+            return far_codes[c][:, g, :].bitcast(FP4X4), far_plane[:, start:start + CHUNK]
+
+        def gene_major_pass(bank, b, g, operand):
+            lhsT, lhsT_scale = z_block(g, b)
+            rhs, rhs_scale = operand
+            nc.tensor.matmul_mx(out=bank[:], lhsT=lhsT, lhsT_scale=lhsT_scale, rhs=rhs, rhs_scale=rhs_scale,
+                                start=(g == 0), stop=(g == PASSES - 1))
+
+        def by_slot(bank):
+            return bank[:].rearrange("p (m t) -> p t m", t=PACK)
+
+        mid_bank, far_bank, scaled_mid, lag_sum, turned_bank, turned, grouped = {}, {}, {}, {}, {}, {}, {}
+        near_bank, y_bf = {}, {}
+
+        def mid_matmuls(c, b):
+            mid_bank[c, b] = new_bank()
+            for g in range(PASSES):
+                gene_major_pass(mid_bank[c, b], b, g, mid_operand(c, g))
+
+        def far_matmuls(c, b):
+            far_bank[c, b] = new_bank()
+            for g in range(PASSES):
+                gene_major_pass(far_bank[c, b], b, g, far_operand(c, g))
+
+        def scale_mid(c, b):
+            scaled_mid[c, b] = work.tile([P, PACK, P], F32, name="scaled_mid", tag="scaled_mid", bufs=8)
+            nc.scalar.activation(out=scaled_mid[c, b][:], in_=by_slot(mid_bank[c, b]), func=COPY,
+                                 scale=r_mid_col[:, b:b + 1])
+
+        def add_far(c, b):
+            lag_sum[c, b] = work.tile([P, PACK, P], F32, name="lag_sum", tag="lag_sum", bufs=8)
+            nc.vector.scalar_tensor_tensor(out=lag_sum[c, b][:], in0=by_slot(far_bank[c, b]),
+                                           scalar=r_far_raw[:, b, 0:1], in1=scaled_mid[c, b][:],
+                                           op0=MULT, op1=ADD)
+
+        def turn(c):
+            for b in range(BLOCKS):
+                turned_bank[c, b] = new_bank()
+                for t in range(PACK):
+                    nc.tensor.transpose(turned_bank[c, b][:, t * P:(t + 1) * P], lag_sum[c, b][:, t, :], ident[:])
+
+        def copy_turned(c):
+            turned[c] = work.tile([P, PACK, GENES], F32, name="turned", tag="turned", bufs=2)
+            for b in range(BLOCKS):
+                nc.scalar.copy(out=turned[c][:, :, b * P:(b + 1) * P],
+                               in_=turned_bank[c, b][:].rearrange("p (t n) -> p t n", t=PACK))
+
+        def interleave(engine, c, g):
+            grouped[c, g] = work.tile([P, PACK * CHUNK], BF16, name="grouped", tag="grouped", bufs=4, align_bytes=64)
+            dst = grouped[c, g][:].rearrange("p (t m j) -> p m j t", t=PACK, j=PACK)
+            src = near_raw[c, g][:].rearrange("p j (m t) -> p m j t", t=PACK)
+            if engine is nc.scalar:
+                nc.scalar.copy(out=dst, in_=src)
+            else:
+                nc.vector.tensor_copy(out=dst, in_=src)
+
+        def quantise_near(c, g):
+            nc.vector.quantize_mx(out=near_codes[c, g][:].bitcast(FP8X4), scales=near_plane[c, g][:],
+                                  in_=grouped[c, g][:])
+
+        def near_matmuls(c, gene0, width, t0):
+            slots = CHUNK // width
+            bank = new_bank()
+            near_bank[c, gene0, t0] = bank
+            for s in range(slots):
+                t = t0 + s
+                for g in range(PASSES):
+                    nc.tensor.matmul_mx(
+                        out=bank[:, s * width:(s + 1) * width],
+                        lhsT=near_codes[c, g][:, t * P:(t + 1) * P].bitcast(FP8X4),
+                        lhsT_scale=near_plane[c, g][:, t * P:(t + 1) * P],
+                        rhs=z_codes[g][:, gene0:gene0 + width].bitcast(FP8X4),
+                        rhs_scale=z_plane[:, g * GENES + gene0:g * GENES + gene0 + width],
+                        start=(g == 0), stop=(g == PASSES - 1))
+
+        def add_near(c, gene0, width, t0):
+            slots = CHUNK // width
+            nc.vector.tensor_tensor(
+                out=y[c][:, t0:t0 + slots, gene0:gene0 + width],
+                in0=near_bank[c, gene0, t0][:].rearrange("p (s n) -> p s n", s=slots),
+                in1=turned[c][:, t0:t0 + slots, gene0:gene0 + width], op=ADD)
+
+        def store_y(c, gene0, width):
+            nc.sync.dma_start(
+                out=out_0[cols(c), gene0:gene0 + width].rearrange("(p t) m -> p t m", t=PACK),
+                in_=y[c][:, :, gene0:gene0 + width])
+
+        def round_y(engine, c, gene0, width):
+            tile = work.tile([P, PACK * width], BF16, name="y_bf", tag="y_bf", bufs=3, align_bytes=64)
+            y_bf[c, gene0] = tile
+            dst = tile[:].rearrange("p (n i t) -> p n t i", i=4, t=PACK)
+            src = y[c][:, :, gene0:gene0 + width].rearrange("p t (n i) -> p n t i", i=4)
+            if engine is nc.scalar:
+                nc.scalar.copy(out=dst, in_=src)
+            else:
+                nc.vector.tensor_copy(out=dst, in_=src)
+
+        def quantise_y(c, gene0, width):
+            nc.vector.quantize_mx(out=y_codes[:, c, gene0:gene0 + width].bitcast(FP8X4),
+                                  scales=y_plane[:, c, gene0:gene0 + width], in_=y_bf[c, gene0][:])
+
+        def store_codes(c, gene0, width):
+            nc.sync.dma_start(
+                out=out_1[c, :, gene0:gene0 + width, :].rearrange("p m t -> p (m t)").bitcast(I32),
+                in_=y_codes[:, c, gene0:gene0 + width].bitcast(I32))
+
+        ACT, DVE = nc.scalar, nc.vector
+        H = GENES // 2
+        QTR = GENES // 4
+
+        for b in range(BLOCKS):
+            mid_bank[0, b] = new_bank()
+        for g in range(PASSES):
+            for b in range(BLOCKS):
+                gene_major_pass(mid_bank[0, b], b, g, mid_operand(0, g))
+        for b in range(BLOCKS):
+            scale_mid(0, b)
+        for b in range(BLOCKS):
+            far_matmuls(0, b)
+            add_far(0, b)
+        interleave(ACT, 0, 0)
+        for b in range(BLOCKS):
+            mid_matmuls(1, b)
+            scale_mid(1, b)
+        interleave(DVE, 0, 1)
+        quantise_near(0, 0)
+        interleave(DVE, 0, 2)
+        quantise_near(0, 1)
+        quantise_near(0, 2)
+        turn(0)
+        copy_turned(0)
+        for b in range(BLOCKS):
+            far_matmuls(1, b)
+            add_far(1, b)
+        interleave(ACT, 1, 0)
+        interleave(ACT, 1, 1)
+        interleave(ACT, 1, 2)
+        quantise_near(1, 0)
+        for gene0 in (0, H):
+            for t0 in (0, 2):
+                near_matmuls(0, gene0, H, t0)
+        add_near(0, 0, H, 0)
+        add_near(0, 0, H, 2)
+        store_y(0, 0, H)
+        add_near(0, H, H, 0)
+        round_y(DVE, 0, 0, H)
+        add_near(0, H, H, 2)
+        store_y(0, H, H)
+        quantise_y(0, 0, H)
+        store_codes(0, 0, H)
+        round_y(DVE, 0, H, H)
+        quantise_near(1, 1)
+        quantise_y(0, H, H)
+        store_codes(0, H, H)
+        for b in range(BLOCKS):
+            mid_matmuls(2, b)
+            scale_mid(2, b)
+        interleave(DVE, 2, 0)
+        quantise_near(1, 2)
+        interleave(DVE, 2, 1)
+        quantise_near(2, 0)
+        turn(1)
+        copy_turned(1)
+        for b in range(BLOCKS):
+            far_matmuls(2, b)
+            add_far(2, b)
+        quantise_near(2, 1)
+        interleave(ACT, 2, 2)
+        for gene0 in (0, H):
+            for t0 in (0, 2):
+                near_matmuls(1, gene0, H, t0)
+        add_near(1, 0, H, 0)
+        add_near(1, 0, H, 2)
+        store_y(1, 0, H)
+        round_y(ACT, 1, 0, H)
+        quantise_near(2, 2)
+        add_near(1, H, H, 0)
+        add_near(1, H, H, 2)
+        store_y(1, H, H)
+        quantise_y(1, 0, H)
+        store_codes(1, 0, H)
+        round_y(DVE, 1, H, H)
+        turn(2)
+        copy_turned(2)
+        near_matmuls(2, 0, H, 0)
+        near_matmuls(2, 0, H, 2)
+        near_matmuls(2, H, QTR, 0)
+        near_matmuls(2, H + QTR, QTR, 0)
+        add_near(2, 0, H, 0)
+        quantise_y(1, H, H)
+        store_codes(1, H, H)
+        add_near(2, 0, H, 2)
+        store_y(2, 0, H)
+        round_y(ACT, 2, 0, H)
+        add_near(2, H, QTR, 0)
+        store_y(2, H, QTR)
+        round_y(ACT, 2, H, QTR)
+        add_near(2, H + QTR, QTR, 0)
+        store_y(2, H + QTR, QTR)
+        quantise_y(2, 0, H)
+        store_codes(2, 0, H)
+        round_y(DVE, 2, H + QTR, QTR)
+        quantise_y(2, H, QTR)
+        store_codes(2, H, QTR)
+        quantise_y(2, H + QTR, QTR)
+        store_codes(2, H + QTR, QTR)
+        for q in range(QUADS):
+            queue = nc.scalar if q % 2 == 0 else nc.sync
+            queue.dma_start(
+                out=out_2[:, 4 * q:4 * q + 4, :].rearrange("g r n -> r g n").bitcast(I32),
+                in_=y_plane[32 * q:32 * q + 4, :, :].bitcast(I32))

@@ -45,9 +45,9 @@ def tile_moran_three_range_lag_k3_kernel(
             return psum.tile([P, CHUNK], F32, name="bank", tag="bank")
 
         z_codes = [keep_tile([P, GENES], U32, f"z_codes{g}") for g in range(PASSES)]
-        mid_first = [keep_tile([P, CHUNK], U32, f"mid_first{g}") for g in range(PASSES)]
-        mid_later = [keep_tile([P, PASSES, CHUNK], U32, f"mid_later{c}") for c in range(1, CHUNKS)]
-        far_codes = [keep_tile([P, PASSES, 2 * CHUNK], U8, f"far_codes{c}") for c in range(CHUNKS)]
+        far_first = [keep_tile([P, 2 * CHUNK], U8, f"far_first{g}") for g in range(PASSES)]
+        far_later = [keep_tile([P, PASSES, 2 * CHUNK], U8, f"far_later{c}") for c in range(1, CHUNKS)]
+        mid_codes = [keep_tile([P, PASSES, CHUNK], U32, f"mid_codes{c}") for c in range(CHUNKS)]
         near_raw = {(c, g): keep_tile([P, PACK, CHUNK], BF16, f"near_raw{c}{g}")
                     for c in range(CHUNKS) for g in range(PASSES)}
         near_codes = {(c, g): keep_tile([P, CHUNK], U32, f"near_codes{c}{g}")
@@ -57,11 +57,12 @@ def tile_moran_three_range_lag_k3_kernel(
         z_plane = keep_tile([P, PASSES * GENES], U8, "z_plane")
         mid_plane_first = keep_tile([P, PASSES * CHUNK], U8, "mid_plane_first")
         later = SPOTS - CHUNK
-        mid_plane_later = keep_tile([P, PASSES * later], U8, "mid_plane_later")
-        far_plane = keep_tile([P, PASSES * SPOTS], U8, "far_plane")
-        r_mid_raw = keep_tile([P, BLOCKS, 2], BF16, "r_mid_raw")
-        r_far_raw = keep_tile([P, BLOCKS, 2], BF16, "r_far_raw")
-        r_mid_col = keep_tile([P, BLOCKS], F32, "r_mid_col")
+        mid_plane_later = keep_tile([P, PASSES * later + 64], U8, "mid_plane_later")
+        far_plane_first = keep_tile([P, PASSES * CHUNK], U8, "far_plane_first")
+        far_plane_later = keep_tile([P, PASSES * later + 64], U8, "far_plane_later")
+        r_rows = keep_tile([P, P], BF16, "r_rows")
+        r_cols = keep_tile([P, P], BF16, "r_cols")
+        r_far_col = keep_tile([P, BLOCKS], F32, "r_far_col")
         ident = keep_tile([P, P], F32, "ident")
         y_codes = keep_tile([P, CHUNKS, GENES], U32, "y_codes")
         y_plane = keep_tile([P, CHUNKS, GENES], U8, "y_plane")
@@ -70,82 +71,89 @@ def tile_moran_three_range_lag_k3_kernel(
         def cols(c):
             return slice(c * CHUNK, (c + 1) * CHUNK)
 
-        def load_plane(queue, plane, first_row, scales, col0, width, quads):
-            for q in quads:
-                row = 32 * q + first_row
-                queue.dma_start(
-                    out=plane[row:row + 4, 0:PASSES * width].rearrange("r (g n) -> r g n", g=PASSES).bitcast(I32),
-                    in_=scales[:, 4 * q:4 * q + 4, col0:col0 + width].rearrange("g r n -> r g n").bitcast(I32),
+        def load_plane(plane, first_row, scales, col0, width):
+            for r in range(4):
+                nc.sync.dma_start(
+                    out=plane[first_row + r:P:32, 0:PASSES * width].rearrange("q (g n) -> q g n", g=PASSES).bitcast(I32),
+                    in_=scales[:, r:16:4, col0:col0 + width].rearrange("g q n -> q g n").bitcast(I32),
                 )
 
-        def load_z(queue, g):
-            queue.dma_start(out=z_codes[g][:].bitcast(I32),
-                            in_=z_words[g].rearrange("p n t -> p (n t)").bitcast(I32))
+        def load_z(g):
+            nc.sync.dma_start(out=z_codes[g][:].bitcast(I32),
+                              in_=z_words[g].rearrange("p n t -> p (n t)").bitcast(I32))
 
-        def load_mid_first(queue, g):
-            queue.dma_start(out=mid_first[g][:].bitcast(I32),
-                            in_=mid_words[g, :, cols(0), :].rearrange("p n t -> p (n t)").bitcast(I32))
-
-        def load_mid(c):
-            nc.sync.dma_start(out=mid_later[c - 1][:].bitcast(I32),
-                              in_=mid_words[:, :, cols(c), :].rearrange("g p n t -> p g (n t)").bitcast(I32))
+        def load_far_first(g):
+            nc.sync.dma_start(out=far_first[g][:].bitcast(I32), in_=far_words[g, :, 0:2 * CHUNK].bitcast(I32))
 
         def load_far(c):
-            nc.sync.dma_start(out=far_codes[c][:].bitcast(I32),
+            nc.sync.dma_start(out=far_later[c - 1][:].bitcast(I32),
                               in_=far_words[:, :, 2 * CHUNK * c:2 * CHUNK * (c + 1)].rearrange("g p b -> p g b").bitcast(I32))
+
+        def load_mid(c):
+            nc.sync.dma_start(out=mid_codes[c][:].bitcast(I32),
+                              in_=mid_words[:, :, cols(c), :].rearrange("g p n t -> p g (n t)").bitcast(I32))
 
         def load_near(c, g):
             nc.sync.dma_start(out=near_raw[c, g][:],
                               in_=near[cols(g), cols(c)].rearrange("(p j) w -> p j w", j=PACK))
 
         nc.vector.memset(z_plane[:].bitcast(I32), 0)
+        nc.vector.memset(far_plane_first[:].bitcast(I32), 0)
+        nc.vector.memset(r_rows[:], 0.0)
         nc.vector.memset(mid_plane_first[:].bitcast(I32), 0)
-        nc.vector.memset(far_plane[:, 0:PASSES * SPOTS].bitcast(I32), 0)
-        nc.vector.memset(mid_plane_later[:, 0:PASSES * later].bitcast(I32), 0)
+        nc.vector.memset(far_plane_later[:, 0:PASSES * later + 4].bitcast(I32), 0)
+        nc.vector.memset(mid_plane_later[:, 0:PASSES * later + 4].bitcast(I32), 0)
 
-        with nc.allow_non_contiguous_dma(reason="one range weight to a partition"):
-            nc.gpsimd.dma_start(out=r_mid_raw[:, :, 0], in_=r_mid.rearrange("(b p) -> p b", p=P))
-            nc.gpsimd.dma_start(out=r_far_raw[:, :, 0], in_=r_far.rearrange("(b p) -> p b", p=P))
+        nc.gpsimd.dma_start(out=r_rows[0:P:32, :].rearrange("q (b x) -> q b x", b=BLOCKS),
+                            in_=r_far.rearrange("(b q x) -> q b x", b=BLOCKS, q=QUADS))
+        nc.gpsimd.dma_start(out=r_rows[1:P:32, :].rearrange("q (b x) -> q b x", b=BLOCKS),
+                            in_=r_mid.rearrange("(b q x) -> q b x", b=BLOCKS, q=QUADS))
         make_identity(nc, ident[:])
 
-        load_plane(nc.sync, z_plane, 0, z_scales, 0, GENES, range(4))
-        load_z(nc.sync, 0)
-        load_mid_first(nc.sync, 0)
-        load_plane(nc.sync, mid_plane_first, MID_ROW, mid_scales, 0, CHUNK, range(4))
+        load_plane(z_plane, 0, z_scales, 0, GENES)
+        load_z(0)
+        load_far_first(0)
+        load_plane(far_plane_first, 0, far_scales, 0, CHUNK)
         for g in range(1, PASSES):
-            load_z(nc.sync, g)
-            load_mid_first(nc.sync, g)
-        load_plane(nc.sync, far_plane, 0, far_scales, 0, SPOTS, range(4))
-        load_far(0)
+            load_z(g)
+            load_far_first(g)
+        load_mid(0)
+        load_plane(mid_plane_first, MID_ROW, mid_scales, 0, CHUNK)
         load_near(0, 0)
-        load_mid(1)
-        load_plane(nc.sync, mid_plane_later, MID_ROW, mid_scales, CHUNK, later, range(4))
+        load_far(1)
+        load_plane(far_plane_later, 0, far_scales, CHUNK, later)
         load_near(0, 1)
         load_near(0, 2)
-        load_far(1)
-        for g in range(PASSES):
-            load_near(1, g)
-        load_mid(2)
-        load_near(2, 0)
-        load_near(2, 1)
+        load_mid(1)
+        load_plane(mid_plane_later, MID_ROW, mid_scales, CHUNK, later)
+        load_near(1, 0)
+        load_near(1, 1)
+        load_near(1, 2)
         load_far(2)
+        load_near(2, 0)
+        load_mid(2)
+        load_near(2, 1)
         load_near(2, 2)
 
-        nc.scalar.copy(out=r_mid_col[:], in_=r_mid_raw[:, :, 0])
+        nc.vector.transpose(r_cols[:], r_rows[:])
+        nc.scalar.copy(out=r_far_col[:], in_=r_cols[:, 0:P:32])
 
         def z_block(g, b):
             return (z_codes[g][:, b * P:(b + 1) * P].bitcast(FP8X4),
                     z_plane[:, g * GENES + b * P:g * GENES + (b + 1) * P])
 
         def mid_operand(c, g):
+            codes = mid_codes[c][:, g, :].bitcast(FP8X4)
             if c == 0:
-                return mid_first[g][:].bitcast(FP8X4), mid_plane_first[MID_ROW:P, g * CHUNK:(g + 1) * CHUNK]
+                return codes, mid_plane_first[MID_ROW:P, g * CHUNK:(g + 1) * CHUNK]
             start = g * later + (c - 1) * CHUNK
-            return mid_later[c - 1][:, g, :].bitcast(FP8X4), mid_plane_later[MID_ROW:P, start:start + CHUNK]
+            return codes, mid_plane_later[MID_ROW:P, start:start + CHUNK]
 
         def far_operand(c, g):
-            start = g * SPOTS + c * CHUNK
-            return far_codes[c][:, g, :].bitcast(FP4X4), far_plane[:, start:start + CHUNK]
+            if c == 0:
+                return far_first[g][:].bitcast(FP4X4), far_plane_first[:, g * CHUNK:(g + 1) * CHUNK]
+            start = g * later + (c - 1) * CHUNK
+            return far_later[c - 1][:, g, :].bitcast(FP4X4), far_plane_later[:, start:start + CHUNK]
 
         def gene_major_pass(bank, b, g, operand):
             lhsT, lhsT_scale = z_block(g, b)
@@ -156,7 +164,7 @@ def tile_moran_three_range_lag_k3_kernel(
         def by_slot(bank):
             return bank[:].rearrange("p (m t) -> p t m", t=PACK)
 
-        mid_bank, far_bank, scaled_mid, lag_sum, turned_bank, turned, grouped = {}, {}, {}, {}, {}, {}, {}
+        mid_bank, far_bank, scaled_far, lag_sum, turned_bank, turned, grouped = {}, {}, {}, {}, {}, {}, {}
         near_bank, y_bf = {}, {}
 
         def mid_matmuls(c, b):
@@ -169,15 +177,15 @@ def tile_moran_three_range_lag_k3_kernel(
             for g in range(PASSES):
                 gene_major_pass(far_bank[c, b], b, g, far_operand(c, g))
 
-        def scale_mid(c, b):
-            scaled_mid[c, b] = work.tile([P, PACK, P], F32, name="scaled_mid", tag="scaled_mid", bufs=8)
-            nc.scalar.activation(out=scaled_mid[c, b][:], in_=by_slot(mid_bank[c, b]), func=COPY,
-                                 scale=r_mid_col[:, b:b + 1])
+        def scale_far(c, b):
+            scaled_far[c, b] = work.tile([P, PACK, P], F32, name="scaled_far", tag="scaled_far", bufs=8)
+            nc.scalar.activation(out=scaled_far[c, b][:], in_=by_slot(far_bank[c, b]), func=COPY,
+                                 scale=r_far_col[:, b:b + 1])
 
-        def add_far(c, b):
+        def add_mid(c, b):
             lag_sum[c, b] = work.tile([P, PACK, P], F32, name="lag_sum", tag="lag_sum", bufs=8)
-            nc.vector.scalar_tensor_tensor(out=lag_sum[c, b][:], in0=by_slot(far_bank[c, b]),
-                                           scalar=r_far_raw[:, b, 0:1], in1=scaled_mid[c, b][:],
+            nc.vector.scalar_tensor_tensor(out=lag_sum[c, b][:], in0=by_slot(mid_bank[c, b]),
+                                           scalar=r_cols[:, 32 * b + 1:32 * b + 2], in1=scaled_far[c, b][:],
                                            op0=MULT, op1=ADD)
 
         def turn(c):
@@ -255,20 +263,31 @@ def tile_moran_three_range_lag_k3_kernel(
         H = GENES // 2
         QTR = GENES // 4
 
+        def far_phase(c):
+            for b in range(BLOCKS):
+                far_matmuls(c, b)
+                scale_far(c, b)
+
+        def mid_phase(c):
+            for b in range(BLOCKS):
+                mid_matmuls(c, b)
+                add_mid(c, b)
+
+        def near_phase(c):
+            for gene0 in (0, H):
+                for t0 in (0, 2):
+                    near_matmuls(c, gene0, H, t0)
+
         for b in range(BLOCKS):
-            mid_bank[0, b] = new_bank()
+            far_bank[0, b] = new_bank()
         for g in range(PASSES):
             for b in range(BLOCKS):
-                gene_major_pass(mid_bank[0, b], b, g, mid_operand(0, g))
+                gene_major_pass(far_bank[0, b], b, g, far_operand(0, g))
         for b in range(BLOCKS):
-            scale_mid(0, b)
-        for b in range(BLOCKS):
-            far_matmuls(0, b)
-            add_far(0, b)
+            scale_far(0, b)
+        mid_phase(0)
         interleave(ACT, 0, 0)
-        for b in range(BLOCKS):
-            mid_matmuls(1, b)
-            scale_mid(1, b)
+        far_phase(1)
         interleave(DVE, 0, 1)
         quantise_near(0, 0)
         interleave(DVE, 0, 2)
@@ -276,16 +295,11 @@ def tile_moran_three_range_lag_k3_kernel(
         quantise_near(0, 2)
         turn(0)
         copy_turned(0)
-        for b in range(BLOCKS):
-            far_matmuls(1, b)
-            add_far(1, b)
+        mid_phase(1)
         interleave(ACT, 1, 0)
         interleave(ACT, 1, 1)
-        interleave(ACT, 1, 2)
         quantise_near(1, 0)
-        for gene0 in (0, H):
-            for t0 in (0, 2):
-                near_matmuls(0, gene0, H, t0)
+        near_phase(0)
         add_near(0, 0, H, 0)
         add_near(0, 0, H, 2)
         store_y(0, 0, H)
@@ -299,31 +313,26 @@ def tile_moran_three_range_lag_k3_kernel(
         quantise_near(1, 1)
         quantise_y(0, H, H)
         store_codes(0, H, H)
-        for b in range(BLOCKS):
-            mid_matmuls(2, b)
-            scale_mid(2, b)
+        far_phase(2)
+        interleave(DVE, 1, 2)
         interleave(DVE, 2, 0)
         quantise_near(1, 2)
-        interleave(DVE, 2, 1)
         quantise_near(2, 0)
         turn(1)
         copy_turned(1)
-        for b in range(BLOCKS):
-            far_matmuls(2, b)
-            add_far(2, b)
-        quantise_near(2, 1)
+        mid_phase(2)
+        interleave(ACT, 2, 1)
         interleave(ACT, 2, 2)
-        for gene0 in (0, H):
-            for t0 in (0, 2):
-                near_matmuls(1, gene0, H, t0)
+        near_phase(1)
         add_near(1, 0, H, 0)
+        quantise_near(2, 1)
         add_near(1, 0, H, 2)
         store_y(1, 0, H)
-        round_y(ACT, 1, 0, H)
-        quantise_near(2, 2)
         add_near(1, H, H, 0)
+        round_y(DVE, 1, 0, H)
         add_near(1, H, H, 2)
         store_y(1, H, H)
+        quantise_near(2, 2)
         quantise_y(1, 0, H)
         store_codes(1, 0, H)
         round_y(DVE, 1, H, H)
@@ -351,8 +360,8 @@ def tile_moran_three_range_lag_k3_kernel(
         store_codes(2, H, QTR)
         quantise_y(2, H + QTR, QTR)
         store_codes(2, H + QTR, QTR)
-        for q in range(QUADS):
-            queue = nc.scalar if q % 2 == 0 else nc.sync
+        for r in range(4):
+            queue = nc.scalar if r % 2 == 0 else nc.sync
             queue.dma_start(
-                out=out_2[:, 4 * q:4 * q + 4, :].rearrange("g r n -> r g n").bitcast(I32),
-                in_=y_plane[32 * q:32 * q + 4, :, :].bitcast(I32))
+                out=out_2[:, r:16:4, :].rearrange("g q n -> q g n").bitcast(I32),
+                in_=y_plane[r:P:32, :, :].bitcast(I32))

@@ -44,9 +44,9 @@ def tile_moran_three_range_lag_k3_kernel(
         def new_bank():
             return psum.tile([P, CHUNK], F32, name="bank", tag="bank")
 
-        z_codes = [keep_tile([P, GENES], U32, f"z_codes{g}") for g in range(PASSES)]
-        far_first = [keep_tile([P, 2 * CHUNK], U8, f"far_first{g}") for g in range(PASSES)]
-        far_later = [keep_tile([P, PASSES, 2 * CHUNK], U8, f"far_later{c}") for c in range(1, CHUNKS)]
+        z_all = keep_tile([P, PASSES, GENES], U32, "z_all")
+        z_codes = [z_all[:, g, :] for g in range(PASSES)]
+        far_codes = [keep_tile([P, PASSES, 2 * CHUNK], U8, f"far_codes{c}") for c in range(CHUNKS)]
         mid_codes = [keep_tile([P, PASSES, CHUNK], U32, f"mid_codes{c}") for c in range(CHUNKS)]
         near_raw = {(c, g): keep_tile([P, PACK, CHUNK], BF16, f"near_raw{c}{g}")
                     for c in range(CHUNKS) for g in range(PASSES)}
@@ -55,11 +55,8 @@ def tile_moran_three_range_lag_k3_kernel(
         near_plane = {(c, g): keep_tile([P, CHUNK], U8, f"near_plane{c}{g}")
                       for c in range(CHUNKS) for g in range(PASSES)}
         z_plane = keep_tile([P, PASSES * GENES], U8, "z_plane")
-        mid_plane_first = keep_tile([P, PASSES * CHUNK], U8, "mid_plane_first")
-        later = SPOTS - CHUNK
-        mid_plane_later = keep_tile([P, PASSES * later + 64], U8, "mid_plane_later")
-        far_plane_first = keep_tile([P, PASSES * CHUNK], U8, "far_plane_first")
-        far_plane_later = keep_tile([P, PASSES * later + 64], U8, "far_plane_later")
+        mid_plane = [keep_tile([P, PASSES * CHUNK], U8, f"mid_plane{c}") for c in range(CHUNKS)]
+        far_plane = [keep_tile([P, PASSES * CHUNK], U8, f"far_plane{c}") for c in range(CHUNKS)]
         r_rows = keep_tile([P, P], BF16, "r_rows")
         r_cols = keep_tile([P, P], BF16, "r_cols")
         r_far_col = keep_tile([P, BLOCKS], F32, "r_far_col")
@@ -71,38 +68,36 @@ def tile_moran_three_range_lag_k3_kernel(
         def cols(c):
             return slice(c * CHUNK, (c + 1) * CHUNK)
 
-        def load_plane(plane, first_row, scales, col0, width):
+        def load_plane(plane, first_row, scales, c):
             for r in range(4):
                 nc.sync.dma_start(
-                    out=plane[first_row + r:P:32, 0:PASSES * width].rearrange("q (g n) -> q g n", g=PASSES).bitcast(I32),
-                    in_=scales[:, r:16:4, col0:col0 + width].rearrange("g q n -> q g n").bitcast(I32),
+                    out=plane[first_row + r:P:32, :].rearrange("q (g n) -> q g n", g=PASSES).bitcast(I32),
+                    in_=scales[:, r:16:4, cols(c)].rearrange("g q n -> q g n").bitcast(I32),
                 )
 
-        def load_z(g):
-            nc.sync.dma_start(out=z_codes[g][:].bitcast(I32),
-                              in_=z_words[g].rearrange("p n t -> p (n t)").bitcast(I32))
+        def load_z(g0, g1):
+            nc.sync.dma_start(out=z_all[:, g0:g1, :].bitcast(I32),
+                              in_=z_words[g0:g1].rearrange("g p n t -> p g (n t)").bitcast(I32))
 
-        def load_far_first(g):
-            nc.sync.dma_start(out=far_first[g][:].bitcast(I32), in_=far_words[g, :, 0:2 * CHUNK].bitcast(I32))
+        def load_far(c, g0=0, g1=PASSES):
+            nc.sync.dma_start(out=far_codes[c][:, g0:g1, :].bitcast(I32),
+                              in_=far_words[g0:g1, :, 2 * CHUNK * c:2 * CHUNK * (c + 1)].rearrange("g p b -> p g b").bitcast(I32))
 
-        def load_far(c):
-            nc.sync.dma_start(out=far_later[c - 1][:].bitcast(I32),
-                              in_=far_words[:, :, 2 * CHUNK * c:2 * CHUNK * (c + 1)].rearrange("g p b -> p g b").bitcast(I32))
-
-        def load_mid(c):
-            nc.sync.dma_start(out=mid_codes[c][:].bitcast(I32),
-                              in_=mid_words[:, :, cols(c), :].rearrange("g p n t -> p g (n t)").bitcast(I32))
+        def load_mid(c, g0=0, g1=PASSES):
+            nc.sync.dma_start(out=mid_codes[c][:, g0:g1, :].bitcast(I32),
+                              in_=mid_words[g0:g1, :, cols(c), :].rearrange("g p n t -> p g (n t)").bitcast(I32))
 
         def load_near(c, g):
             nc.sync.dma_start(out=near_raw[c, g][:],
                               in_=near[cols(g), cols(c)].rearrange("(p j) w -> p j w", j=PACK))
 
         nc.vector.memset(z_plane[:].bitcast(I32), 0)
-        nc.vector.memset(far_plane_first[:].bitcast(I32), 0)
+        nc.vector.memset(far_plane[0][:].bitcast(I32), 0)
         nc.vector.memset(r_rows[:], 0.0)
-        nc.vector.memset(mid_plane_first[:].bitcast(I32), 0)
-        nc.vector.memset(far_plane_later[:, 0:PASSES * later + 4].bitcast(I32), 0)
-        nc.vector.memset(mid_plane_later[:, 0:PASSES * later + 4].bitcast(I32), 0)
+        nc.vector.memset(mid_plane[0][:].bitcast(I32), 0)
+        for c in range(1, CHUNKS):
+            nc.vector.memset(far_plane[c][:].bitcast(I32), 0)
+            nc.vector.memset(mid_plane[c][:].bitcast(I32), 0)
 
         nc.gpsimd.dma_start(out=r_rows[0:P:32, :].rearrange("q (b x) -> q b x", b=BLOCKS),
                             in_=r_far.rearrange("(b q x) -> q b x", b=BLOCKS, q=QUADS))
@@ -110,30 +105,33 @@ def tile_moran_three_range_lag_k3_kernel(
                             in_=r_mid.rearrange("(b q x) -> q b x", b=BLOCKS, q=QUADS))
         make_identity(nc, ident[:])
 
-        load_plane(z_plane, 0, z_scales, 0, GENES)
-        load_z(0)
-        load_far_first(0)
-        load_plane(far_plane_first, 0, far_scales, 0, CHUNK)
-        for g in range(1, PASSES):
-            load_z(g)
-            load_far_first(g)
-        load_mid(0)
-        load_plane(mid_plane_first, MID_ROW, mid_scales, 0, CHUNK)
+        load_far(0, 0, 1)
+        load_z(0, 1)
+        load_plane(z_plane, 0, z_scales, 0)
+        load_plane(far_plane[0], 0, far_scales, 0)
+        load_far(0, 1, 3)
+        load_z(1, 2)
+        load_z(2, 3)
+        load_plane(mid_plane[0], MID_ROW, mid_scales, 0)
+        load_mid(0, 0, 1)
+        load_mid(0, 1, 3)
         load_near(0, 0)
-        load_far(1)
-        load_plane(far_plane_later, 0, far_scales, CHUNK, later)
         load_near(0, 1)
+        load_plane(far_plane[1], 0, far_scales, 1)
+        load_far(1)
         load_near(0, 2)
-        load_mid(1)
-        load_plane(mid_plane_later, MID_ROW, mid_scales, CHUNK, later)
-        load_near(1, 0)
         load_near(1, 1)
+        load_near(1, 0)
+        load_plane(mid_plane[1], MID_ROW, mid_scales, 1)
+        load_mid(1)
+        load_plane(far_plane[2], 0, far_scales, 2)
+        load_near(2, 0)
         load_near(1, 2)
         load_far(2)
-        load_near(2, 0)
-        load_mid(2)
         load_near(2, 1)
         load_near(2, 2)
+        load_plane(mid_plane[2], MID_ROW, mid_scales, 2)
+        load_mid(2)
 
         nc.vector.transpose(r_cols[:], r_rows[:])
         nc.scalar.copy(out=r_far_col[:], in_=r_cols[:, 0:P:32])
@@ -143,17 +141,10 @@ def tile_moran_three_range_lag_k3_kernel(
                     z_plane[:, g * GENES + b * P:g * GENES + (b + 1) * P])
 
         def mid_operand(c, g):
-            codes = mid_codes[c][:, g, :].bitcast(FP8X4)
-            if c == 0:
-                return codes, mid_plane_first[MID_ROW:P, g * CHUNK:(g + 1) * CHUNK]
-            start = g * later + (c - 1) * CHUNK
-            return codes, mid_plane_later[MID_ROW:P, start:start + CHUNK]
+            return mid_codes[c][:, g, :].bitcast(FP8X4), mid_plane[c][MID_ROW:P, cols(g)]
 
         def far_operand(c, g):
-            if c == 0:
-                return far_first[g][:].bitcast(FP4X4), far_plane_first[:, g * CHUNK:(g + 1) * CHUNK]
-            start = g * later + (c - 1) * CHUNK
-            return far_later[c - 1][:, g, :].bitcast(FP4X4), far_plane_later[:, start:start + CHUNK]
+            return far_codes[c][:, g, :].bitcast(FP4X4), far_plane[c][:, cols(g)]
 
         def gene_major_pass(bank, b, g, operand):
             lhsT, lhsT_scale = z_block(g, b)
@@ -201,22 +192,22 @@ def tile_moran_three_range_lag_k3_kernel(
                                in_=turned_bank[c, b][:].rearrange("p (t n) -> p t n", t=PACK))
 
         def interleave(engine, c, g):
-            grouped[c, g] = work.tile([P, PACK * CHUNK], BF16, name="grouped", tag="grouped", bufs=4, align_bytes=64)
-            dst = grouped[c, g][:].rearrange("p (t m j) -> p m j t", t=PACK, j=PACK)
-            src = near_raw[c, g][:].rearrange("p j (m t) -> p m j t", t=PACK)
+            grouped[c, g] = work.tile([P, PACK * CHUNK], BF16, name="grouped", tag="grouped", bufs=5, align_bytes=64)
             if engine is nc.scalar:
-                nc.scalar.copy(out=dst, in_=src)
+                nc.scalar.copy(out=grouped[c, g][:].rearrange("p (t m j) -> p m j t", t=PACK, j=PACK),
+                               in_=near_raw[c, g][:].rearrange("p j (m t) -> p m j t", t=PACK))
             else:
-                nc.vector.tensor_copy(out=dst, in_=src)
+                nc.vector.tensor_copy(
+                    out=grouped[c, g][:].rearrange("p (t m e j) -> p m t e j", t=PACK, e=2, j=PACK),
+                    in_=near_raw[c, g][:].rearrange("p j (m e t) -> p m t e j", t=PACK, e=2))
 
         def quantise_near(c, g):
             nc.vector.quantize_mx(out=near_codes[c, g][:].bitcast(FP8X4), scales=near_plane[c, g][:],
                                   in_=grouped[c, g][:])
 
-        def near_matmuls(c, gene0, width, t0):
-            slots = CHUNK // width
+        def near_matmuls(c, t0, slots, gene0, width):
             bank = new_bank()
-            near_bank[c, gene0, t0] = bank
+            near_bank[c, t0, gene0] = bank
             for s in range(slots):
                 t = t0 + s
                 for g in range(PASSES):
@@ -228,20 +219,19 @@ def tile_moran_three_range_lag_k3_kernel(
                         rhs_scale=z_plane[:, g * GENES + gene0:g * GENES + gene0 + width],
                         start=(g == 0), stop=(g == PASSES - 1))
 
-        def add_near(c, gene0, width, t0):
-            slots = CHUNK // width
+        def add_near(c, t0, slots, gene0, width):
             nc.vector.tensor_tensor(
                 out=y[c][:, t0:t0 + slots, gene0:gene0 + width],
-                in0=near_bank[c, gene0, t0][:].rearrange("p (s n) -> p s n", s=slots),
+                in0=near_bank[c, t0, gene0][:, 0:slots * width].rearrange("p (s n) -> p s n", s=slots),
                 in1=turned[c][:, t0:t0 + slots, gene0:gene0 + width], op=ADD)
 
-        def store_y(c, gene0, width):
+        def store_y(c, t0, slots, gene0, width):
             nc.sync.dma_start(
-                out=out_0[cols(c), gene0:gene0 + width].rearrange("(p t) m -> p t m", t=PACK),
-                in_=y[c][:, :, gene0:gene0 + width])
+                out=out_0[cols(c), :].rearrange("(p t) m -> p t m", t=PACK)[:, t0:t0 + slots, gene0:gene0 + width],
+                in_=y[c][:, t0:t0 + slots, gene0:gene0 + width])
 
         def round_y(engine, c, gene0, width):
-            tile = work.tile([P, PACK * width], BF16, name="y_bf", tag="y_bf", bufs=3, align_bytes=64)
+            tile = work.tile([P, PACK * width], BF16, name="y_bf", tag="y_bf", bufs=4, align_bytes=64)
             y_bf[c, gene0] = tile
             dst = tile[:].rearrange("p (n i t) -> p n t i", i=4, t=PACK)
             src = y[c][:, :, gene0:gene0 + width].rearrange("p t (n i) -> p n t i", i=4)
@@ -273,10 +263,13 @@ def tile_moran_three_range_lag_k3_kernel(
                 mid_matmuls(c, b)
                 add_mid(c, b)
 
-        def near_phase(c):
-            for gene0 in (0, H):
-                for t0 in (0, 2):
-                    near_matmuls(c, gene0, H, t0)
+        def store_scales(c0, c1):
+            for r in range(4):
+                queue = nc.scalar if r % 2 == 0 and c1 == CHUNKS else nc.sync
+                queue.dma_start(
+                    out=out_2[c0:c1, r:16:4, :].rearrange("g q n -> q g n").bitcast(I32),
+                    in_=y_plane[r:P:32, c0:c1, :].bitcast(I32))
+
 
         for b in range(BLOCKS):
             far_bank[0, b] = new_bank()
@@ -285,83 +278,76 @@ def tile_moran_three_range_lag_k3_kernel(
                 gene_major_pass(far_bank[0, b], b, g, far_operand(0, g))
         for b in range(BLOCKS):
             scale_far(0, b)
-        mid_phase(0)
         interleave(ACT, 0, 0)
-        far_phase(1)
+        mid_phase(0)
+        turn(0)
         interleave(DVE, 0, 1)
         quantise_near(0, 0)
         interleave(DVE, 0, 2)
+        copy_turned(0)
+        far_phase(1)
         quantise_near(0, 1)
         quantise_near(0, 2)
-        turn(0)
-        copy_turned(0)
-        mid_phase(1)
+        interleave(DVE, 1, 1)
         interleave(ACT, 1, 0)
-        interleave(ACT, 1, 1)
-        quantise_near(1, 0)
-        near_phase(0)
-        add_near(0, 0, H, 0)
-        add_near(0, 0, H, 2)
-        store_y(0, 0, H)
-        add_near(0, H, H, 0)
-        round_y(DVE, 0, 0, H)
-        add_near(0, H, H, 2)
-        store_y(0, H, H)
-        quantise_y(0, 0, H)
-        store_codes(0, 0, H)
-        round_y(DVE, 0, H, H)
-        quantise_near(1, 1)
-        quantise_y(0, H, H)
-        store_codes(0, H, H)
-        far_phase(2)
-        interleave(DVE, 1, 2)
-        interleave(DVE, 2, 0)
-        quantise_near(1, 2)
-        quantise_near(2, 0)
+        for t in range(PACK):
+            near_matmuls(0, t, 1, 0, GENES)
+            add_near(0, t, 1, 0, GENES)
+            if t == 0:
+                quantise_near(1, 1)
+        store_y(0, 0, PACK, 0, GENES)
+        interleave(ACT, 2, 0)
+        mid_phase(1)
         turn(1)
         copy_turned(1)
-        mid_phase(2)
-        interleave(ACT, 2, 1)
+        round_y(DVE, 0, 0, H)
+        quantise_near(1, 0)
+        interleave(DVE, 1, 2)
+        round_y(ACT, 0, H, H)
+        quantise_near(2, 0)
+        quantise_near(1, 2)
+        interleave(DVE, 2, 1)
+        far_phase(2)
+        quantise_y(0, 0, H)
+        quantise_y(0, H, H)
+        store_codes(0, 0, GENES)
         interleave(ACT, 2, 2)
-        near_phase(1)
-        add_near(1, 0, H, 0)
-        quantise_near(2, 1)
-        add_near(1, 0, H, 2)
-        store_y(1, 0, H)
-        add_near(1, H, H, 0)
-        round_y(DVE, 1, 0, H)
-        add_near(1, H, H, 2)
-        store_y(1, H, H)
-        quantise_near(2, 2)
-        quantise_y(1, 0, H)
-        store_codes(1, 0, H)
-        round_y(DVE, 1, H, H)
+        for t in range(PACK):
+            near_matmuls(1, t, 1, 0, GENES)
+            add_near(1, t, 1, 0, GENES)
+            if t == 1:
+                quantise_near(2, 1)
+                store_y(1, 0, 2, 0, GENES)
+        store_y(1, 2, 2, 0, GENES)
+        round_y(ACT, 1, 0, H)
+        mid_phase(2)
         turn(2)
         copy_turned(2)
-        near_matmuls(2, 0, H, 0)
-        near_matmuls(2, 0, H, 2)
-        near_matmuls(2, H, QTR, 0)
-        near_matmuls(2, H + QTR, QTR, 0)
-        add_near(2, 0, H, 0)
+        quantise_near(2, 2)
+        round_y(DVE, 1, H, H)
+        quantise_y(1, 0, H)
         quantise_y(1, H, H)
-        store_codes(1, H, H)
-        add_near(2, 0, H, 2)
-        store_y(2, 0, H)
+        store_codes(1, 0, GENES)
+        store_scales(0, 2)
+        near_matmuls(2, 0, 2, 0, H)
+        near_matmuls(2, 2, 2, 0, H)
+        near_matmuls(2, 0, 2, H, H)
+        near_matmuls(2, 2, 2, H, QTR)
+        near_matmuls(2, 2, 2, H + QTR, QTR)
+        add_near(2, 0, 2, 0, H)
+        add_near(2, 2, 2, 0, H)
+        store_y(2, 2, 2, 0, H)
         round_y(ACT, 2, 0, H)
-        add_near(2, H, QTR, 0)
-        store_y(2, H, QTR)
+        add_near(2, 0, 2, H, H)
+        store_y(2, 0, 2, 0, GENES)
+        add_near(2, 2, 2, H, QTR)
         round_y(ACT, 2, H, QTR)
-        add_near(2, H + QTR, QTR, 0)
-        store_y(2, H + QTR, QTR)
+        add_near(2, 2, 2, H + QTR, QTR)
+        store_y(2, 2, 2, H, H)
         quantise_y(2, 0, H)
         store_codes(2, 0, H)
         round_y(DVE, 2, H + QTR, QTR)
         quantise_y(2, H, QTR)
-        store_codes(2, H, QTR)
         quantise_y(2, H + QTR, QTR)
-        store_codes(2, H + QTR, QTR)
-        for r in range(4):
-            queue = nc.scalar if r % 2 == 0 else nc.sync
-            queue.dma_start(
-                out=out_2[:, r:16:4, :].rearrange("g q n -> q g n").bitcast(I32),
-                in_=y_plane[r:P:32, :, :].bitcast(I32))
+        store_codes(2, H, H)
+        store_scales(2, CHUNKS)

from contextlib import ExitStack

import concourse.mybir as mybir
from concourse.masks import make_identity

SPOTS, GENES = 1536, 512
FLOPS = 3 * 2 * SPOTS * SPOTS * GENES

F32 = mybir.dt.float32
BF16 = mybir.dt.bfloat16
I32 = mybir.dt.int32
U32 = mybir.dt.uint32
U8 = mybir.dt.uint8
FP8X4 = mybir.dt.float8_e4m3fn_x4
FP4X4 = mybir.dt.float4_e2m1fn_x4
COPY = mybir.ActivationFunctionType.Copy
MULT = mybir.AluOpType.mult
ADD = mybir.AluOpType.add

P = 128
PACK = 4
CHUNK = P * PACK
PASSES = SPOTS // CHUNK
CHUNKS = SPOTS // CHUNK
BLOCKS = GENES // P
QUADS = 4
MID_ROW = 4


def tile_moran_three_range_lag_k3_kernel(
    tc, z_words, z_scales, near, mid_words, mid_scales, far_words, far_scales, r_mid, r_far,
    out_0, out_1, out_2,
):
    nc = tc.nc
    with ExitStack() as ctx:
        keep = ctx.enter_context(tc.tile_pool(name="keep", bufs=1))
        work = ctx.enter_context(tc.tile_pool(name="work", bufs=2))
        psum = ctx.enter_context(tc.psum_pool(name="psum", bufs=8))
        ctx.enter_context(tc.manual_schedule())

        def keep_tile(shape, dtype, name):
            return keep.tile(shape, dtype, name=name, align_bytes=64)

        def new_bank():
            return psum.tile([P, CHUNK], F32, name="bank", tag="bank")

        z_all = keep_tile([P, PASSES, GENES], U32, "z_all")
        z_codes = [z_all[:, g, :] for g in range(PASSES)]
        far_codes = [keep_tile([P, PASSES, 2 * CHUNK], U8, f"far_codes{c}") for c in range(CHUNKS)]
        mid_codes = [keep_tile([P, PASSES, CHUNK], U32, f"mid_codes{c}") for c in range(CHUNKS)]
        near_raw = {(c, g): keep_tile([P, PACK, CHUNK], BF16, f"near_raw{c}{g}")
                    for c in range(CHUNKS) for g in range(PASSES)}
        near_codes = {(c, g): keep_tile([P, CHUNK], U32, f"near_codes{c}{g}")
                      for c in range(CHUNKS) for g in range(PASSES)}
        near_plane = {(c, g): keep_tile([P, CHUNK], U8, f"near_plane{c}{g}")
                      for c in range(CHUNKS) for g in range(PASSES)}
        z_plane = keep_tile([P, PASSES * GENES], U8, "z_plane")
        mid_plane = [keep_tile([P, PASSES * CHUNK], U8, f"mid_plane{c}") for c in range(CHUNKS)]
        far_plane = [keep_tile([P, PASSES * CHUNK], U8, f"far_plane{c}") for c in range(CHUNKS)]
        r_rows = keep_tile([P, P], BF16, "r_rows")
        r_cols = keep_tile([P, P], BF16, "r_cols")
        r_far_col = keep_tile([P, BLOCKS], F32, "r_far_col")
        ident = keep_tile([P, P], F32, "ident")
        y_codes = keep_tile([P, CHUNKS, GENES], U32, "y_codes")
        y_plane = keep_tile([P, CHUNKS, GENES], U8, "y_plane")
        y = [keep_tile([P, PACK, GENES], F32, f"y{c}") for c in range(CHUNKS)]

        def cols(c):
            return slice(c * CHUNK, (c + 1) * CHUNK)

        def load_plane(plane, first_row, scales, c):
            for r in range(4):
                nc.sync.dma_start(
                    out=plane[first_row + r:P:32, :].rearrange("q (g n) -> q g n", g=PASSES).bitcast(I32),
                    in_=scales[:, r:16:4, cols(c)].rearrange("g q n -> q g n").bitcast(I32),
                )

        def load_z(g0, g1):
            nc.sync.dma_start(out=z_all[:, g0:g1, :].bitcast(I32),
                              in_=z_words[g0:g1].rearrange("g p n t -> p g (n t)").bitcast(I32))

        def load_far(c, g0=0, g1=PASSES):
            nc.sync.dma_start(out=far_codes[c][:, g0:g1, :].bitcast(I32),
                              in_=far_words[g0:g1, :, 2 * CHUNK * c:2 * CHUNK * (c + 1)].rearrange("g p b -> p g b").bitcast(I32))

        def load_mid(c, g0=0, g1=PASSES):
            nc.sync.dma_start(out=mid_codes[c][:, g0:g1, :].bitcast(I32),
                              in_=mid_words[g0:g1, :, cols(c), :].rearrange("g p n t -> p g (n t)").bitcast(I32))

        def load_near(c, g):
            nc.sync.dma_start(out=near_raw[c, g][:],
                              in_=near[cols(g), cols(c)].rearrange("(p j) w -> p j w", j=PACK))

        nc.vector.memset(z_plane[:].bitcast(I32), 0)
        nc.vector.memset(far_plane[0][:].bitcast(I32), 0)
        nc.vector.memset(r_rows[:], 0.0)
        nc.vector.memset(mid_plane[0][:].bitcast(I32), 0)
        for c in range(1, CHUNKS):
            nc.vector.memset(far_plane[c][:].bitcast(I32), 0)
            nc.vector.memset(mid_plane[c][:].bitcast(I32), 0)

        nc.gpsimd.dma_start(out=r_rows[0:P:32, :].rearrange("q (b x) -> q b x", b=BLOCKS),
                            in_=r_far.rearrange("(b q x) -> q b x", b=BLOCKS, q=QUADS))
        nc.gpsimd.dma_start(out=r_rows[1:P:32, :].rearrange("q (b x) -> q b x", b=BLOCKS),
                            in_=r_mid.rearrange("(b q x) -> q b x", b=BLOCKS, q=QUADS))
        make_identity(nc, ident[:])

        load_far(0, 0, 1)
        load_z(0, 1)
        load_plane(z_plane, 0, z_scales, 0)
        load_plane(far_plane[0], 0, far_scales, 0)
        load_far(0, 1, 3)
        load_z(1, 2)
        load_z(2, 3)
        load_plane(mid_plane[0], MID_ROW, mid_scales, 0)
        load_mid(0, 0, 1)
        load_mid(0, 1, 3)
        load_near(0, 0)
        load_near(0, 1)
        load_plane(far_plane[1], 0, far_scales, 1)
        load_far(1)
        load_near(0, 2)
        load_near(1, 1)
        load_near(1, 0)
        load_plane(mid_plane[1], MID_ROW, mid_scales, 1)
        load_mid(1)
        load_plane(far_plane[2], 0, far_scales, 2)
        load_near(2, 0)
        load_near(1, 2)
        load_far(2)
        load_near(2, 1)
        load_near(2, 2)
        load_plane(mid_plane[2], MID_ROW, mid_scales, 2)
        load_mid(2)

        nc.vector.transpose(r_cols[:], r_rows[:])
        nc.scalar.copy(out=r_far_col[:], in_=r_cols[:, 0:P:32])

        def z_block(g, b):
            return (z_codes[g][:, b * P:(b + 1) * P].bitcast(FP8X4),
                    z_plane[:, g * GENES + b * P:g * GENES + (b + 1) * P])

        def mid_operand(c, g):
            return mid_codes[c][:, g, :].bitcast(FP8X4), mid_plane[c][MID_ROW:P, cols(g)]

        def far_operand(c, g):
            return far_codes[c][:, g, :].bitcast(FP4X4), far_plane[c][:, cols(g)]

        def gene_major_pass(bank, b, g, operand):
            lhsT, lhsT_scale = z_block(g, b)
            rhs, rhs_scale = operand
            nc.tensor.matmul_mx(out=bank[:], lhsT=lhsT, lhsT_scale=lhsT_scale, rhs=rhs, rhs_scale=rhs_scale,
                                start=(g == 0), stop=(g == PASSES - 1))

        def by_slot(bank):
            return bank[:].rearrange("p (m t) -> p t m", t=PACK)

        mid_bank, far_bank, scaled_far, lag_sum, turned_bank, turned, grouped = {}, {}, {}, {}, {}, {}, {}
        near_bank, y_bf = {}, {}

        def mid_matmuls(c, b):
            mid_bank[c, b] = new_bank()
            for g in range(PASSES):
                gene_major_pass(mid_bank[c, b], b, g, mid_operand(c, g))

        def far_matmuls(c, b):
            far_bank[c, b] = new_bank()
            for g in range(PASSES):
                gene_major_pass(far_bank[c, b], b, g, far_operand(c, g))

        def scale_far(c, b):
            scaled_far[c, b] = work.tile([P, PACK, P], F32, name="scaled_far", tag="scaled_far", bufs=8)
            nc.scalar.activation(out=scaled_far[c, b][:], in_=by_slot(far_bank[c, b]), func=COPY,
                                 scale=r_far_col[:, b:b + 1])

        def add_mid(c, b):
            lag_sum[c, b] = work.tile([P, PACK, P], F32, name="lag_sum", tag="lag_sum", bufs=8)
            nc.vector.scalar_tensor_tensor(out=lag_sum[c, b][:], in0=by_slot(mid_bank[c, b]),
                                           scalar=r_cols[:, 32 * b + 1:32 * b + 2], in1=scaled_far[c, b][:],
                                           op0=MULT, op1=ADD)

        def turn(c):
            for b in range(BLOCKS):
                turned_bank[c, b] = new_bank()
                for t in range(PACK):
                    nc.tensor.transpose(turned_bank[c, b][:, t * P:(t + 1) * P], lag_sum[c, b][:, t, :], ident[:])

        def copy_turned(c):
            turned[c] = work.tile([P, PACK, GENES], F32, name="turned", tag="turned", bufs=2)
            for b in range(BLOCKS):
                nc.scalar.copy(out=turned[c][:, :, b * P:(b + 1) * P],
                               in_=turned_bank[c, b][:].rearrange("p (t n) -> p t n", t=PACK))

        def interleave(engine, c, g):
            grouped[c, g] = work.tile([P, PACK * CHUNK], BF16, name="grouped", tag="grouped", bufs=5, align_bytes=64)
            if engine is nc.scalar:
                nc.scalar.copy(out=grouped[c, g][:].rearrange("p (t m j) -> p m j t", t=PACK, j=PACK),
                               in_=near_raw[c, g][:].rearrange("p j (m t) -> p m j t", t=PACK))
            else:
                nc.vector.tensor_copy(
                    out=grouped[c, g][:].rearrange("p (t m e j) -> p m t e j", t=PACK, e=2, j=PACK),
                    in_=near_raw[c, g][:].rearrange("p j (m e t) -> p m t e j", t=PACK, e=2))

        def quantise_near(c, g):
            nc.vector.quantize_mx(out=near_codes[c, g][:].bitcast(FP8X4), scales=near_plane[c, g][:],
                                  in_=grouped[c, g][:])

        def near_matmuls(c, t0, slots, gene0, width):
            bank = new_bank()
            near_bank[c, t0, gene0] = bank
            for s in range(slots):
                t = t0 + s
                for g in range(PASSES):
                    nc.tensor.matmul_mx(
                        out=bank[:, s * width:(s + 1) * width],
                        lhsT=near_codes[c, g][:, t * P:(t + 1) * P].bitcast(FP8X4),
                        lhsT_scale=near_plane[c, g][:, t * P:(t + 1) * P],
                        rhs=z_codes[g][:, gene0:gene0 + width].bitcast(FP8X4),
                        rhs_scale=z_plane[:, g * GENES + gene0:g * GENES + gene0 + width],
                        start=(g == 0), stop=(g == PASSES - 1))

        def add_near(c, t0, slots, gene0, width):
            nc.vector.tensor_tensor(
                out=y[c][:, t0:t0 + slots, gene0:gene0 + width],
                in0=near_bank[c, t0, gene0][:, 0:slots * width].rearrange("p (s n) -> p s n", s=slots),
                in1=turned[c][:, t0:t0 + slots, gene0:gene0 + width], op=ADD)

        def store_y(c, t0, slots, gene0, width):
            nc.sync.dma_start(
                out=out_0[cols(c), :].rearrange("(p t) m -> p t m", t=PACK)[:, t0:t0 + slots, gene0:gene0 + width],
                in_=y[c][:, t0:t0 + slots, gene0:gene0 + width])

        def round_y(engine, c, gene0, width):
            tile = work.tile([P, PACK * width], BF16, name="y_bf", tag="y_bf", bufs=4, align_bytes=64)
            y_bf[c, gene0] = tile
            dst = tile[:].rearrange("p (n i t) -> p n t i", i=4, t=PACK)
            src = y[c][:, :, gene0:gene0 + width].rearrange("p t (n i) -> p n t i", i=4)
            if engine is nc.scalar:
                nc.scalar.copy(out=dst, in_=src)
            else:
                nc.vector.tensor_copy(out=dst, in_=src)

        def quantise_y(c, gene0, width):
            nc.vector.quantize_mx(out=y_codes[:, c, gene0:gene0 + width].bitcast(FP8X4),
                                  scales=y_plane[:, c, gene0:gene0 + width], in_=y_bf[c, gene0][:])

        def store_codes(c, gene0, width):
            nc.sync.dma_start(
                out=out_1[c, :, gene0:gene0 + width, :].rearrange("p m t -> p (m t)").bitcast(I32),
                in_=y_codes[:, c, gene0:gene0 + width].bitcast(I32))

        ACT, DVE = nc.scalar, nc.vector
        H = GENES // 2
        QTR = GENES // 4

        def far_phase(c):
            for b in range(BLOCKS):
                far_matmuls(c, b)
                scale_far(c, b)

        def mid_phase(c):
            for b in range(BLOCKS):
                mid_matmuls(c, b)
                add_mid(c, b)

        def store_scales(c0, c1):
            for r in range(4):
                queue = nc.scalar if r % 2 == 0 and c1 == CHUNKS else nc.sync
                queue.dma_start(
                    out=out_2[c0:c1, r:16:4, :].rearrange("g q n -> q g n").bitcast(I32),
                    in_=y_plane[r:P:32, c0:c1, :].bitcast(I32))


        for b in range(BLOCKS):
            far_bank[0, b] = new_bank()
        for g in range(PASSES):
            for b in range(BLOCKS):
                gene_major_pass(far_bank[0, b], b, g, far_operand(0, g))
        for b in range(BLOCKS):
            scale_far(0, b)
        interleave(ACT, 0, 0)
        mid_phase(0)
        turn(0)
        interleave(DVE, 0, 1)
        quantise_near(0, 0)
        interleave(DVE, 0, 2)
        copy_turned(0)
        far_phase(1)
        quantise_near(0, 1)
        quantise_near(0, 2)
        interleave(DVE, 1, 1)
        interleave(ACT, 1, 0)
        for t in range(PACK):
            near_matmuls(0, t, 1, 0, GENES)
            add_near(0, t, 1, 0, GENES)
            if t == 0:
                quantise_near(1, 1)
        store_y(0, 0, PACK, 0, GENES)
        interleave(ACT, 2, 0)
        mid_phase(1)
        turn(1)
        copy_turned(1)
        round_y(DVE, 0, 0, H)
        quantise_near(1, 0)
        interleave(DVE, 1, 2)
        round_y(ACT, 0, H, H)
        quantise_near(2, 0)
        quantise_near(1, 2)
        interleave(DVE, 2, 1)
        far_phase(2)
        quantise_y(0, 0, H)
        quantise_y(0, H, H)
        store_codes(0, 0, GENES)
        interleave(ACT, 2, 2)
        for t in range(PACK):
            near_matmuls(1, t, 1, 0, GENES)
            add_near(1, t, 1, 0, GENES)
            if t == 1:
                quantise_near(2, 1)
                store_y(1, 0, 2, 0, GENES)
        store_y(1, 2, 2, 0, GENES)
        round_y(ACT, 1, 0, H)
        mid_phase(2)
        turn(2)
        copy_turned(2)
        quantise_near(2, 2)
        round_y(DVE, 1, H, H)
        quantise_y(1, 0, H)
        quantise_y(1, H, H)
        store_codes(1, 0, GENES)
        store_scales(0, 2)
        near_matmuls(2, 0, 2, 0, H)
        near_matmuls(2, 2, 2, 0, H)
        near_matmuls(2, 0, 2, H, H)
        near_matmuls(2, 2, 2, H, QTR)
        near_matmuls(2, 2, 2, H + QTR, QTR)
        add_near(2, 0, 2, 0, H)
        add_near(2, 2, 2, 0, H)
        store_y(2, 2, 2, 0, H)
        round_y(ACT, 2, 0, H)
        add_near(2, 0, 2, H, H)
        store_y(2, 0, 2, 0, GENES)
        add_near(2, 2, 2, H, QTR)
        round_y(ACT, 2, H, QTR)
        add_near(2, 2, 2, H + QTR, QTR)
        store_y(2, 2, 2, H, H)
        quantise_y(2, 0, H)
        store_codes(2, 0, H)
        round_y(DVE, 2, H + QTR, QTR)
        quantise_y(2, H, QTR)
        quantise_y(2, H + QTR, QTR)
        store_codes(2, H, H)
        store_scales(2, CHUNKS)
